import numpy as np
import ml_dtypes

BF16 = ml_dtypes.bfloat16


def bf(x):
    return np.asarray(x, np.float32).astype(BF16)


def f32(x):
    return np.asarray(x, np.float32)


def f64(x):
    return np.asarray(x).astype(np.float64)


def striped(idx):
    return np.tile(idx.reshape(-1, 16).T, (8, 1))


S, K, M, N = 512, 128, 512, 192


def setup_inputs():
    return {"table": bf(np.random.standard_normal((K, S))), "w": bf(np.random.standard_normal((K, M)) / np.sqrt(K)), "u": f32(np.random.standard_normal((M, N))), "offs": striped(np.random.permutation(S)[:N])}


def reference(table, w, u, offs):
    idx = offs[:16].T.reshape(-1)
    x = f64(table)[:, idx]
    y = f64(w).T @ x
    return y * f64(u)

@@ -1,0 +1,47 @@
+import concourse.mybir as mybir
+
+BF16, F32, U16 = mybir.dt.bfloat16, mybir.dt.float32, mybir.dt.uint16
+
+P = 128
+S = 512
+M = 512
+N = 192
+BLOCKS = M // P
+
+FLOPS = 2 * P * M * N
+BYTES = 2 * P * N + 2 * P * M + 4 * M * N + 2 * P * (N // 16) + 4 * M * N
+
+
+def tile_gather_matmul_kernel(tc, table, w, u, offs, out):
+    nc = tc.nc
+    with (
+        tc.tile_pool(name="held", bufs=1) as held,
+        tc.psum_pool(name="banks", bufs=1) as banks,
+    ):
+        offsets = held.tile([P, N // 16], U16, name="offsets")
+        nc.sync.dma_start(offsets[:], offs)
+        store = held.tile([P, S], BF16, name="store")
+        nc.sync.dma_start(store[:], table)
+        weights = held.tile([P, M], BF16, name="weights")
+        nc.scalar.dma_start(weights[:], w)
+
+        queues = [nc.sync, nc.scalar]
+
+        factors = []
+        for b in range(BLOCKS):
+            factor = held.tile([P, N], F32, name="factor%d" % b)
+            queues[b % 2].dma_start(factor[:], u[b * P : (b + 1) * P, :])
+            factors.append(factor)
+
+        for b in range(BLOCKS):
+            layer = banks.tile([P, N], F32, name="layer%d" % b)
+            nc.tensor.matmul(
+                layer[:],
+                weights[:, b * P : (b + 1) * P],
+                store[:].indirect(offsets[:]),
+                start=True,
+                stop=True,
+            )
+            result = held.tile([P, N], F32, name="result%d" % b)
+            nc.vector.tensor_tensor(result[:], layer[:], factors[b][:], mybir.AluOpType.mult)
+            queues[b % 2].dma_start(out[b * P : (b + 1) * P, :], result[:])

@@ -7,6 +7,8 @@ S = 512
 M = 512
 N = 192
 BLOCKS = M // P
+BANK = 512
+WARM_UPS = 4
 
 FLOPS = 2 * P * M * N
 BYTES = 2 * P * N + 2 * P * M + 4 * M * N + 2 * P * (N // 16) + 4 * M * N
@@ -24,6 +26,18 @@ def tile_gather_matmul_kernel(tc, table, w, u, offs, out):
         nc.sync.dma_start(store[:], table)
         weights = held.tile([P, M], BF16, name="weights")
         nc.scalar.dma_start(weights[:], w)
+
+        zeros = held.tile([P, P], BF16, name="zeros")
+        nc.vector.memset(zeros[:], 0.0)
+        unused = banks.tile([P, BANK // P, P], F32, name="unused")
+        for i in range(WARM_UPS):
+            nc.tensor.matmul(
+                unused[:],
+                zeros[:],
+                zeros[:].unsqueeze(1).to_broadcast([P, BANK // P, P]),
+                start=True,
+                stop=True,
+            )
 
         queues = [nc.sync, nc.scalar]
 

@@ -6,7 +6,8 @@ P = 128
 S = 512
 M = 512
 N = 192
-BLOCKS = M // P
+TURNS = M // P
+PAIR = 2
 BANK = 512
 WARM_UPS = 4
 
@@ -16,6 +17,8 @@ BYTES = 2 * P * N + 2 * P * M + 4 * M * N + 2 * P * (N // 16) + 4 * M * N
 
 def tile_gather_matmul_kernel(tc, table, w, u, offs, out):
     nc = tc.nc
+    u_turns = u.rearrange("(p a) n -> p a n", a=TURNS)
+    out_turns = out.rearrange("(p a) n -> p a n", a=TURNS)
     with (
         tc.tile_pool(name="held", bufs=1) as held,
         tc.psum_pool(name="banks", bufs=1) as banks,
@@ -39,23 +42,29 @@ def tile_gather_matmul_kernel(tc, table, w, u, offs, out):
                 stop=True,
             )
 
+        sorted_weights = held.tile([P, TURNS, P], BF16, name="sorted_weights")
+        for a in range(TURNS):
+            nc.vector.tensor_copy(sorted_weights[:, a, :], weights[:, a::TURNS])
+
         queues = [nc.sync, nc.scalar]
 
         factors = []
-        for b in range(BLOCKS):
-            factor = held.tile([P, N], F32, name="factor%d" % b)
-            queues[b % 2].dma_start(factor[:], u[b * P : (b + 1) * P, :])
+        for h in range(TURNS // PAIR):
+            factor = held.tile([P, PAIR, N], F32, name="factor%d" % h)
+            queues[h].dma_start(factor[:], u_turns[:, h * PAIR : (h + 1) * PAIR, :])
             factors.append(factor)
 
-        for b in range(BLOCKS):
-            layer = banks.tile([P, N], F32, name="layer%d" % b)
-            nc.tensor.matmul(
-                layer[:],
-                weights[:, b * P : (b + 1) * P],
-                store[:].indirect(offsets[:]),
-                start=True,
-                stop=True,
-            )
-            result = held.tile([P, N], F32, name="result%d" % b)
-            nc.vector.tensor_tensor(result[:], layer[:], factors[b][:], mybir.AluOpType.mult)
-            queues[b % 2].dma_start(out[b * P : (b + 1) * P, :], result[:])
+        for h in range(TURNS // PAIR):
+            result = held.tile([P, PAIR, N], F32, name="result%d" % h)
+            for i in range(PAIR):
+                a = h * PAIR + i
+                layer = banks.tile([P, N], F32, name="layer%d" % a)
+                nc.tensor.matmul(
+                    layer[:],
+                    sorted_weights[:, a, :],
+                    store[:].indirect(offsets[:]),
+                    start=True,
+                    stop=True,
+                )
+                nc.vector.tensor_tensor(result[:, i, :], layer[:], factors[h][:, i, :], mybir.AluOpType.mult)
+            queues[h].dma_start(out_turns[:, h * PAIR : (h + 1) * PAIR, :], result[:])

@@ -25,10 +25,10 @@ def tile_gather_matmul_kernel(tc, table, w, u, offs, out):
     ):
         offsets = held.tile([P, N // 16], U16, name="offsets")
         nc.sync.dma_start(offsets[:], offs)
+        weights = held.tile([P, M], BF16, name="weights")
+        nc.sync.dma_start(weights[:], w)
         store = held.tile([P, S], BF16, name="store")
         nc.sync.dma_start(store[:], table)
-        weights = held.tile([P, M], BF16, name="weights")
-        nc.scalar.dma_start(weights[:], w)
 
         zeros = held.tile([P, P], BF16, name="zeros")
         nc.vector.memset(zeros[:], 0.0)
@@ -46,13 +46,13 @@ def tile_gather_matmul_kernel(tc, table, w, u, offs, out):
         for a in range(TURNS):
             nc.vector.tensor_copy(sorted_weights[:, a, :], weights[:, a::TURNS])
 
-        queues = [nc.sync, nc.scalar]
-
         factors = []
         for h in range(TURNS // PAIR):
             factor = held.tile([P, PAIR, N], F32, name="factor%d" % h)
-            queues[h].dma_start(factor[:], u_turns[:, h * PAIR : (h + 1) * PAIR, :])
+            nc.sync.dma_start(factor[:], u_turns[:, h * PAIR : (h + 1) * PAIR, :])
             factors.append(factor)
+
+        queues = [nc.sync, nc.scalar]
 
         for h in range(TURNS // PAIR):
             result = held.tile([P, PAIR, N], F32, name="result%d" % h)

@@ -52,8 +52,6 @@ def tile_gather_matmul_kernel(tc, table, w, u, offs, out):
             nc.sync.dma_start(factor[:], u_turns[:, h * PAIR : (h + 1) * PAIR, :])
             factors.append(factor)
 
-        queues = [nc.sync, nc.scalar]
-
         for h in range(TURNS // PAIR):
             result = held.tile([P, PAIR, N], F32, name="result%d" % h)
             for i in range(PAIR):
@@ -67,4 +65,4 @@ def tile_gather_matmul_kernel(tc, table, w, u, offs, out):
                     stop=True,
                 )
                 nc.vector.tensor_tensor(result[:, i, :], layer[:], factors[h][:, i, :], mybir.AluOpType.mult)
-            queues[h].dma_start(out_turns[:, h * PAIR : (h + 1) * PAIR, :], result[:])
+            nc.sync.dma_start(out_turns[:, h * PAIR : (h + 1) * PAIR, :], result[:])

@@ -8,6 +8,7 @@ M = 512
 N = 192
 TURNS = M // P
 PAIR = 2
+STORES = [(0, 2), (2, 3), (3, 4)]
 BANK = 512
 WARM_UPS = 4
 
@@ -52,17 +53,17 @@ def tile_gather_matmul_kernel(tc, table, w, u, offs, out):
             nc.sync.dma_start(factor[:], u_turns[:, h * PAIR : (h + 1) * PAIR, :])
             factors.append(factor)
 
-        for h in range(TURNS // PAIR):
-            result = held.tile([P, PAIR, N], F32, name="result%d" % h)
-            for i in range(PAIR):
-                a = h * PAIR + i
-                layer = banks.tile([P, N], F32, name="layer%d" % a)
-                nc.tensor.matmul(
-                    layer[:],
-                    sorted_weights[:, a, :],
-                    store[:].indirect(offsets[:]),
-                    start=True,
-                    stop=True,
-                )
-                nc.vector.tensor_tensor(result[:, i, :], layer[:], factors[h][:, i, :], mybir.AluOpType.mult)
-            nc.sync.dma_start(out_turns[:, h * PAIR : (h + 1) * PAIR, :], result[:])
+        result = held.tile([P, TURNS, N], F32, name="result")
+        for a in range(TURNS):
+            layer = banks.tile([P, N], F32, name="layer%d" % a)
+            nc.tensor.matmul(
+                layer[:],
+                sorted_weights[:, a, :],
+                store[:].indirect(offsets[:]),
+                start=True,
+                stop=True,
+            )
+            nc.vector.tensor_tensor(result[:, a, :], layer[:], factors[a // PAIR][:, a % PAIR, :], mybir.AluOpType.mult)
+            for first, end in STORES:
+                if end == a + 1:
+                    nc.sync.dma_start(out_turns[:, first:end, :], result[:, first:end, :])

@@ -9,8 +9,6 @@ N = 192
 TURNS = M // P
 PAIR = 2
 STORES = [(0, 2), (2, 3), (3, 4)]
-BANK = 512
-WARM_UPS = 4
 
 FLOPS = 2 * P * M * N
 BYTES = 2 * P * N + 2 * P * M + 4 * M * N + 2 * P * (N // 16) + 4 * M * N
@@ -30,18 +28,6 @@ def tile_gather_matmul_kernel(tc, table, w, u, offs, out):
         nc.sync.dma_start(weights[:], w)
         store = held.tile([P, S], BF16, name="store")
         nc.sync.dma_start(store[:], table)
-
-        zeros = held.tile([P, P], BF16, name="zeros")
-        nc.vector.memset(zeros[:], 0.0)
-        unused = banks.tile([P, BANK // P, P], F32, name="unused")
-        for i in range(WARM_UPS):
-            nc.tensor.matmul(
-                unused[:],
-                zeros[:],
-                zeros[:].unsqueeze(1).to_broadcast([P, BANK // P, P]),
-                start=True,
-                stop=True,
-            )
 
         sorted_weights = held.tile([P, TURNS, P], BF16, name="sorted_weights")
         for a in range(TURNS):

@@ -22,10 +22,10 @@ def tile_gather_matmul_kernel(tc, table, w, u, offs, out):
         tc.tile_pool(name="held", bufs=1) as held,
         tc.psum_pool(name="banks", bufs=1) as banks,
     ):
-        offsets = held.tile([P, N // 16], U16, name="offsets")
-        nc.sync.dma_start(offsets[:], offs)
         weights = held.tile([P, M], BF16, name="weights")
         nc.sync.dma_start(weights[:], w)
+        offsets = held.tile([P, N // 16], U16, name="offsets")
+        nc.sync.dma_start(offsets[:], offs)
         store = held.tile([P, S], BF16, name="store")
         nc.sync.dma_start(store[:], table)
 

@@ -8,6 +8,7 @@ M = 512
 N = 192
 TURNS = M // P
 PAIR = 2
+BURST = 256
 STORES = [(0, 2), (2, 3), (3, 4)]
 
 FLOPS = 2 * P * M * N
@@ -22,11 +23,11 @@ def tile_gather_matmul_kernel(tc, table, w, u, offs, out):
         tc.tile_pool(name="held", bufs=1) as held,
         tc.psum_pool(name="banks", bufs=1) as banks,
     ):
-        weights = held.tile([P, M], BF16, name="weights")
+        weights = held.tile([P, M], BF16, name="weights", align_bytes=BURST)
         nc.sync.dma_start(weights[:], w)
         offsets = held.tile([P, N // 16], U16, name="offsets")
         nc.sync.dma_start(offsets[:], offs)
-        store = held.tile([P, S], BF16, name="store")
+        store = held.tile([P, S], BF16, name="store", align_bytes=BURST)
         nc.sync.dma_start(store[:], table)
 
         sorted_weights = held.tile([P, TURNS, P], BF16, name="sorted_weights")
@@ -35,11 +36,11 @@ def tile_gather_matmul_kernel(tc, table, w, u, offs, out):
 
         factors = []
         for h in range(TURNS // PAIR):
-            factor = held.tile([P, PAIR, N], F32, name="factor%d" % h)
+            factor = held.tile([P, PAIR, N], F32, name="factor%d" % h, align_bytes=BURST)
             nc.sync.dma_start(factor[:], u_turns[:, h * PAIR : (h + 1) * PAIR, :])
             factors.append(factor)
 
-        result = held.tile([P, TURNS, N], F32, name="result")
+        result = held.tile([P, TURNS, N], F32, name="result", align_bytes=BURST)
         for a in range(TURNS):
             layer = banks.tile([P, N], F32, name="layer%d" % a)
             nc.tensor.matmul(

@@ -8,7 +8,7 @@ M = 512
 N = 192
 TURNS = M // P
 PAIR = 2
-BURST = 256
+BURST = 1024
 STORES = [(0, 2), (2, 3), (3, 4)]
 
 FLOPS = 2 * P * M * N

import concourse.mybir as mybir

BF16, F32, U16 = mybir.dt.bfloat16, mybir.dt.float32, mybir.dt.uint16

P = 128
S = 512
M = 512
N = 192
TURNS = M // P
PAIR = 2
BURST = 1024
STORES = [(0, 2), (2, 3), (3, 4)]

FLOPS = 2 * P * M * N
BYTES = 2 * P * N + 2 * P * M + 4 * M * N + 2 * P * (N // 16) + 4 * M * N


def tile_gather_matmul_kernel(tc, table, w, u, offs, out):
    nc = tc.nc
    u_turns = u.rearrange("(p a) n -> p a n", a=TURNS)
    out_turns = out.rearrange("(p a) n -> p a n", a=TURNS)
    with (
        tc.tile_pool(name="held", bufs=1) as held,
        tc.psum_pool(name="banks", bufs=1) as banks,
    ):
        weights = held.tile([P, M], BF16, name="weights", align_bytes=BURST)
        nc.sync.dma_start(weights[:], w)
        offsets = held.tile([P, N // 16], U16, name="offsets")
        nc.sync.dma_start(offsets[:], offs)
        store = held.tile([P, S], BF16, name="store", align_bytes=BURST)
        nc.sync.dma_start(store[:], table)

        sorted_weights = held.tile([P, TURNS, P], BF16, name="sorted_weights")
        for a in range(TURNS):
            nc.vector.tensor_copy(sorted_weights[:, a, :], weights[:, a::TURNS])

        factors = []
        for h in range(TURNS // PAIR):
            factor = held.tile([P, PAIR, N], F32, name="factor%d" % h, align_bytes=BURST)
            nc.sync.dma_start(factor[:], u_turns[:, h * PAIR : (h + 1) * PAIR, :])
            factors.append(factor)

        result = held.tile([P, TURNS, N], F32, name="result", align_bytes=BURST)
        for a in range(TURNS):
            layer = banks.tile([P, N], F32, name="layer%d" % a)
            nc.tensor.matmul(
                layer[:],
                sorted_weights[:, a, :],
                store[:].indirect(offsets[:]),
                start=True,
                stop=True,
            )
            nc.vector.tensor_tensor(result[:, a, :], layer[:], factors[a // PAIR][:, a % PAIR, :], mybir.AluOpType.mult)
            for first, end in STORES:
                if end == a + 1:
                    nc.sync.dma_start(out_turns[:, first:end, :], result[:, first:end, :])
